import numpy as np
import ml_dtypes


def mxq(x, axis, fmt="e4m3"):
    dtype, down = {"e4m3": (ml_dtypes.float8_e4m3fn, 7), "e5m2": (ml_dtypes.float8_e5m2, 14)}[fmt]
    v = np.moveaxis(np.asarray(x, np.float32).astype(ml_dtypes.bfloat16).astype(np.float64), axis, -1)
    blocks = v.reshape(v.shape[:-1] + (-1, 32))
    amax = np.abs(blocks).max(-1, keepdims=True)
    byte = np.maximum(np.where(amax > 0, np.frexp(amax)[1] - 1 + 127, 0) - down, 1)
    scale = np.exp2(byte - 127.0)
    codes = (blocks / scale).astype(np.float32).astype(dtype).astype(np.float64)
    return np.moveaxis((codes * scale).reshape(v.shape), -1, axis)


WIDE = False


def mx_kscale(k):
    if not WIDE:
        return np.ones(k)
    levels = np.array([10, -10, 5, -5, 0])
    if k % 512:
        return np.exp2(np.random.permutation(np.resize(levels, k // 32))).repeat(32)
    a = np.empty((k // 512, 16))
    for p in range(k // 512):
        a[p, :8] = np.random.permutation(np.resize(levels, 8))
        for g in range(8):
            far = levels[np.abs(levels - a[p, g]) >= 10]
            a[p, g + 8] = far[np.random.randint(len(far))]
    return np.exp2(a.ravel()).repeat(32)


def f64(x):
    return np.asarray(x).astype(np.float64)


def striped(idx):
    return np.tile(idx.reshape(-1, 16).T, (8, 1)).astype(np.uint16)


def unstriped(offs):
    return offs[:16].T.reshape(-1).astype(np.int64)


E2M1 = np.array([0.0, 0.5, 1.0, 1.5, 2.0, 3.0, 4.0, 6.0, -0.0, -0.5, -1.0, -1.5, -2.0, -3.0, -4.0, -6.0])


def pack_weight(w, fmt):
    k, n = w.shape
    w = f64(np.asarray(w, np.float32).astype(ml_dtypes.bfloat16)).reshape(k // 32, 32, n)
    amax = np.abs(w).max(1)
    if fmt == "e4m3":
        byte = np.frexp(amax)[1] - 1 + 127 - 7
    else:
        mant, ex = np.frexp(amax / 6.0)
        byte = np.where(mant > 0.5, ex, ex - 1) + 127
    byte = np.clip(np.where(amax > 0, byte, 1), 1, 254)
    scaled = (w * np.exp2(127.0 - byte)[:, None, :]).reshape(k, n).astype(np.float32)
    by_word = np.ascontiguousarray(scaled.reshape(k // 512, 128, 4, n).transpose(0, 1, 3, 2))
    if fmt == "e4m3":
        words = by_word.astype(ml_dtypes.float8_e4m3fn).view(np.uint8)
    else:
        c = by_word.astype(ml_dtypes.float4_e2m1fn).view(np.uint8) & 0xF
        words = (c[..., 0::2] | (c[..., 1::2] << 4)).reshape(k // 512, 128, 2 * n)
    return np.ascontiguousarray(words), np.ascontiguousarray(byte.astype(np.uint8).reshape(k // 512, 16, n))


def unpack_weight(words, scales, fmt):
    g, _, n = scales.shape
    words = np.ascontiguousarray(words).reshape(g, 128, n, -1)
    if fmt == "e4m3":
        vals = words.view(ml_dtypes.float8_e4m3fn).astype(np.float64)
    else:
        nib = np.empty((g, 128, n, 4), np.uint8)
        nib[..., 0::2] = words & 0xF
        nib[..., 1::2] = words >> 4
        vals = E2M1[nib]
    vals = vals * np.repeat(np.exp2(scales.astype(np.float64) - 127.0), 8, axis=1)[..., None]
    return vals.transpose(0, 1, 3, 2).reshape(g * 512, n)


def gelu(v):
    return 0.5 * v * (1.0 + np.tanh(np.sqrt(2.0 / np.pi) * (v + 0.044715 * v**3)))


K, T, S, S2 = 1024, 2048, 512, 1024


def setup_inputs():
    n = np.random.standard_normal
    s = mx_kscale(K)[:, None]
    d = {}
    d["tab_words"], d["tab_scales"] = pack_weight(n((K, T)) * s, "e4m3")
    d["offs"] = striped(np.random.permutation(T)[:S])
    d["offs2"] = striped(np.random.permutation(T)[:S2])
    d["w1"] = (n((K, K)) / K / s / s.T).astype(np.float32)
    d["w2_words"], d["w2_scales"] = pack_weight(n((K, K)) / K / s / s.T, "e2m1")
    d["w3_words"], d["w3_scales"] = pack_weight(n((K, K)) / K / s / s.T, "e4m3")
    d["duties"] = (1.5 * np.exp(0.5 * n((S2, S)))).astype(np.float32)
    return d


def reference(tab_words, tab_scales, offs, offs2, w1, w2_words, w2_scales,
              w3_words, w3_scales, duties):
    TW = unpack_weight(tab_words, tab_scales, "e4m3")
    v = TW[:, unstriped(offs)]
    v2 = TW[:, unstriped(offs2)]
    h1 = mxq(f64(w1), 0, "e4m3").T @ v
    h2 = unpack_weight(w2_words, w2_scales, "e2m1").T @ v
    h3 = unpack_weight(w3_words, w3_scales, "e4m3").T @ v
    f = np.maximum(np.abs(h1) - h2, 0.0)
    fq = mxq(f, 0, "e4m3")
    hq = mxq(h3, 0, "e4m3")
    e = v2.T @ fq + v2.T @ hq
    return np.log(1.0 + np.abs(f64(duties) * e))

@@ -1,0 +1,305 @@
+from contextlib import ExitStack
+
+import concourse.mybir as mybir
+
+K, T, S, S2 = 1024, 2048, 512, 1024
+FLOPS = 2 * K * K * S * 3 + 2 * S2 * K * S * 2
+
+F32 = mybir.dt.float32
+BF16 = mybir.dt.bfloat16
+I32 = mybir.dt.int32
+U32 = mybir.dt.uint32
+U16 = mybir.dt.uint16
+U8 = mybir.dt.uint8
+FP8X4 = mybir.dt.float8_e4m3fn_x4
+FP4X4 = mybir.dt.float4_e2m1fn_x4
+ACT = mybir.ActivationFunctionType
+ALU = mybir.AluOpType
+
+P = 128
+PACK = 4
+PASS = P * PACK
+PASSES = K // PASS
+QUADS = 4
+CHUNK = 128
+HALF = 256
+
+
+def tile_list_winter_crew_friction_kernel(
+    tc, tab_words, tab_scales, offs, offs2, w1, w2_words, w2_scales, w3_words, w3_scales, duties, out
+):
+    nc = tc.nc
+    with ExitStack() as ctx:
+        lists = ctx.enter_context(tc.tile_pool(name="lists", bufs=1))
+        keep = ctx.enter_context(tc.tile_pool(name="keep", bufs=1))
+        ring = ctx.enter_context(tc.tile_pool(name="ring", bufs=3))
+        psum = ctx.enter_context(tc.psum_pool(name="psum", bufs=4))
+
+        def held(shape, dtype, name, tag=""):
+            return keep.tile(shape, dtype, name=name, tag=tag or name, align_bytes=64)
+
+        cand_list = lists.tile([P, S // 16], U16, name="cand_list")
+        crew_list = lists.tile([P, S2 // 16], U16, name="crew_list")
+        tab_w = [held([P, T], I32, f"tab_w{a}") for a in range(PASSES)]
+        tab_s = held([P, T], U8, "tab_s")
+        ws_raw = held([P, K], U8, "ws_raw")
+        cand_s1 = held([P, S], U8, "cand_s1")
+        w2_s = [held([P, K], U8, f"w2_s{a}") for a in range(PASSES)]
+        warm = held([P, 2], F32, "warm")
+        w1_raw = {}
+        w3_raw = {}
+        w2_raw = {}
+        duty = {}
+
+        nc.vector.memset(tab_s[:].bitcast(I32), 0)
+        nc.vector.memset(ws_raw[:].bitcast(I32), 0)
+        nc.vector.memset(cand_s1[:].bitcast(I32), 0)
+        for a in range(PASSES):
+            nc.vector.memset(w2_s[a][:].bitcast(I32), 0)
+        nc.vector.memset(warm[:, 0:1], 1.0)
+        nc.scalar.activation(out=warm[:, 1:2], in_=warm[:, 0:1], func=ACT.Ln, bias=1.0)
+
+        def load_words(tile, words):
+            nc.sync.dma_start(out=tile, in_=words.rearrange("p n i -> p (n i)").bitcast(I32))
+
+        def load_scales(tile, row, scales):
+            for quad in range(QUADS):
+                nc.sync.dma_start(
+                    out=tile[32 * quad + row : 32 * quad + row + 8, :].bitcast(I32),
+                    in_=scales[:, 4 * quad : 4 * quad + 4, :].bitcast(I32),
+                )
+
+        def load_w3(b, a, tag=""):
+            w3_raw[b, a] = held([P, PASS], I32, f"w3_raw{b}{a}", tag)
+            load_words(w3_raw[b, a][:], w3_words[a][:, PASS * b : PASS * (b + 1), :])
+
+        def load_w2(a):
+            w2_raw[a] = held([P, K // 2], I32, f"w2_raw{a}")
+            nc.sync.dma_start(out=w2_raw[a][:], in_=w2_words[a].bitcast(I32))
+
+        def load_w1(b, a):
+            w1_raw[b, a] = held([P, PACK, PASS], F32, f"w1_raw{b}{a}", f"w1_raw{a}")
+            rows = w1[PASS * a : PASS * (a + 1), PASS * b : PASS * (b + 1)]
+            nc.sync.dma_start(out=w1_raw[b, a][:], in_=rows.rearrange("(p i) c -> p i c", i=PACK))
+
+        def load_duty(g, tag):
+            duty[g] = held([P, 4, S], F32, f"duty{g}", tag)
+            rows = duties[4 * P * g : 4 * P * (g + 1), :]
+            nc.sync.dma_start(out=duty[g][:], in_=rows.rearrange("(u p) j -> p u j", u=4))
+
+        def lower_rows(tile, source, row):
+            nc.sync.dma_start(out=tile[0 : P - row, :].bitcast(I32), in_=source[row:P, :].bitcast(I32))
+
+        nc.sync.dma_start(cand_list[:], offs)
+        for part in range(4):
+            ts = slice(PASS * part, PASS * (part + 1))
+            load_words(tab_w[0][:, ts], tab_words[0][:, ts, :])
+        nc.sync.dma_start(crew_list[:], offs2)
+        load_w1(0, 0)
+        load_w3(0, 0)
+        load_scales(tab_s[:], 0, tab_scales)
+        load_words(tab_w[1][:], tab_words[1])
+        load_scales(ws_raw[:], 0, w3_scales)
+        load_w3(0, 1)
+        load_scales(ws_raw[:], 8, w2_scales)
+        load_w1(0, 1)
+        load_w2(0)
+        load_w2(1)
+
+
+        def gather(name, width, dtype, window, offsets, tag=""):
+            tile = held([P, width], dtype, name, tag)
+            nc.vector.tensor_copy(tile[:], window.indirect(offsets))
+            return tile
+
+        def deal(name, dtype, source):
+            tile = held(list(source.shape), dtype, name)
+            nc.vector.tensor_copy(
+                out=tile[:].rearrange("p (b t m) -> p b m t", m=P, t=PACK),
+                in_=source.rearrange("p (b m t) -> p b m t", m=P, t=PACK),
+            )
+            return tile
+
+        cand_w = [None] * PASSES
+        w3_w = {}
+        cand_w[0] = gather("cand_w0", S, U32, tab_w[0][:].bitcast(U32), cand_list[:])
+        cand_s = gather("cand_s", S, U8, tab_s[:], cand_list[:])
+        lower_rows(cand_s1, cand_s, 4)
+        cand_w[1] = gather("cand_w1", S, U32, tab_w[1][:].bitcast(U32), cand_list[:])
+        ws = deal("ws", U8, ws_raw[:])
+        for a in range(PASSES):
+            lower_rows(w2_s[a], ws, 8 + 4 * a)
+
+        def deal_w3(b):
+            for a in range(PASSES):
+                w3_w[b, a] = deal(f"w3_w{b}{a}", I32, w3_raw[b, a][:])
+
+        def deal_w2():
+            for a in range(PASSES):
+                w2_w[a] = deal(f"w2_w{a}", U16, w2_raw[a][:].bitcast(U16))
+
+        def first_stage(c, weight, moving_scale):
+            bank = psum.tile([P, PACK, CHUNK], F32, name="bank", tag="first")
+            js = slice(CHUNK * c, CHUNK * (c + 1))
+            for t in range(PACK):
+                for a in range(PASSES):
+                    lhs, lhs_scale = weight(a, t)
+                    nc.tensor.matmul_mx(
+                        out=bank[:, t, :], lhsT=lhs, lhsT_scale=lhs_scale,
+                        rhs=cand_w[a][:, js].bitcast(FP8X4), rhs_scale=moving_scale(a, js),
+                        start=(a == 0), stop=(a == PASSES - 1),
+                    )
+            return bank[:].rearrange("p t j -> p j t")
+
+        def packed_cand_scale(a, js):
+            return cand_s[4 * a : P, js]
+
+        def lowered_cand_scale(a, js):
+            return (cand_s, cand_s1)[a][:, js]
+
+        def columns(b, t):
+            return slice(PASS * b + P * t, PASS * b + P * (t + 1))
+
+        def quantise(name, source, width):
+            codes = held([P, width], U32, name + "_w")
+            scales = held([P, width], U8, name + "_s")
+            nc.vector.quantize_mx(out=codes[:].bitcast(FP8X4), scales=scales[:], in_=source)
+            return codes, scales
+
+        h3_q = {}
+        f_q = {}
+        w1_q = {}
+        w2_w = [None] * PASSES
+
+        def linear_part(b, h):
+            rounded = ring.tile([P, HALF, PACK], BF16, name="h3_rounded", align_bytes=64)
+            for cc in range(2):
+                h3 = first_stage(
+                    2 * h + cc,
+                    lambda a, t: (w3_w[b, a][:, columns(0, t)].bitcast(FP8X4), ws[4 * a : P, columns(b, t)]),
+                    packed_cand_scale,
+                )
+                nc.scalar.copy(out=rounded[:, CHUNK * cc : CHUNK * (cc + 1), :], in_=h3)
+            h3_q[b, h] = quantise(f"h3_q{b}{h}", rounded[:].rearrange("p j t -> p (j t)"), HALF)
+
+        def prepare_w1(b, a):
+            grouped = ring.tile([P, PASS * PACK], BF16, name="w1_grouped", align_bytes=64)
+            nc.scalar.copy(
+                out=grouped[:].rearrange("p (t m i) -> p m i t", t=PACK, i=PACK),
+                in_=w1_raw[b, a][:].rearrange("p i (m t) -> p m i t", t=PACK),
+            )
+            w1_q[b, a] = quantise(f"w1_q{b}{a}", grouped[:], PASS)
+
+        sizes = {}
+
+        def size_part(b, h):
+            sizes[b, h] = held([P, HALF, PACK], F32, f"size{b}{h}")
+            for cc in range(2):
+                h1 = first_stage(
+                    2 * h + cc,
+                    lambda a, t: (
+                        w1_q[b, a][0][:, columns(0, t)].bitcast(FP8X4),
+                        w1_q[b, a][1][:, columns(0, t)],
+                    ),
+                    packed_cand_scale,
+                )
+                nc.scalar.activation(out=sizes[b, h][:, CHUNK * cc : CHUNK * (cc + 1), :], in_=h1, func=ACT.Abs)
+
+        def strain(b, h):
+            excess = ring.tile([P, HALF, PACK], BF16, name="excess", align_bytes=64)
+            for cc in range(2):
+                h2 = first_stage(
+                    2 * h + cc,
+                    lambda a, t: (w2_w[a][:, columns(b, t)].bitcast(FP4X4), w2_s[a][:, columns(b, t)]),
+                    lowered_cand_scale,
+                )
+                js = slice(CHUNK * cc, CHUNK * (cc + 1))
+                nc.vector.tensor_tensor(out=excess[:, js, :], in0=sizes[b, h][:, js, :], in1=h2, op=ALU.subtract)
+            clipped = ring.tile([P, HALF * PACK], BF16, name="clipped", align_bytes=64)
+            nc.vector.tensor_scalar(
+                out=clipped[:], in0=excess[:].rearrange("p j t -> p (j t)"), scalar1=0.0, scalar2=None, op0=ALU.max
+            )
+            f_q[b, h] = quantise(f"f_q{b}{h}", clipped[:], HALF)
+
+        crew_w = {}
+        crew_s = {}
+
+        def crew_words(g, a, tag=""):
+            offsets = crew_list[:, 32 * g : 32 * (g + 1)]
+            crew_w[g, a] = gather(f"crew_w{g}{a}", PASS, U32, tab_w[a][:].bitcast(U32), offsets, tag)
+
+        def crew_scales(g, tag=""):
+            crew_s[g] = gather(f"crew_s{g}", PASS, U8, tab_s[:], crew_list[:, 32 * g : 32 * (g + 1)], tag)
+
+        def second_pass(bank, q, operand, b, start, stop):
+            codes, scales = operand
+            for u in range(2):
+                g, place = divmod(2 * q + u, 4)
+                ms = slice(P * place, P * (place + 1))
+                nc.tensor.matmul_mx(
+                    out=bank[:, u, :], lhsT=crew_w[g, b][:, ms].bitcast(FP8X4), lhsT_scale=crew_s[g][4 * b : P, ms],
+                    rhs=codes[:].bitcast(FP8X4), rhs_scale=scales[:],
+                    start=(start and u == 0), stop=(stop and u == 1),
+                )
+
+        def second_early(q, h, tag):
+            bank = psum.tile([P, 2, HALF], F32, name="bank", tag=tag)
+            second_pass(bank, q, f_q[0, h], 0, True, False)
+            second_pass(bank, q, h3_q[0, h], 0, False, False)
+            second_pass(bank, q, h3_q[1, h], 1, False, False)
+            return bank
+
+        def second_late(h, banks):
+            js = slice(HALF * h, HALF * (h + 1))
+            for q in range(4):
+                if h == 1:
+                    banks.append(second_early(q, h, "first"))
+                second_pass(banks[q], q, f_q[1, h], 1, False, True)
+                weighted = ring.tile([P, 2, HALF], F32, name="weighted")
+                nc.vector.tensor_tensor(out=weighted[:], in0=duty[q // 2][:, 2 * (q % 2) : 2 * (q % 2) + 2, js], in1=banks[q][:], op=ALU.mult)
+                positive = ring.tile([P, 2, HALF], F32, name="positive")
+                if q % 2 == 1:
+                    nc.vector.scalar_tensor_tensor(
+                        out=positive[:], in0=weighted[:], scalar=-1.0, in1=weighted[:], op0=ALU.mult, op1=ALU.max
+                    )
+                else:
+                    nc.scalar.activation(out=positive[:], in_=weighted[:], func=ACT.Abs)
+                result = ring.tile([P, 2, HALF], F32, name="result", bufs=8)
+                nc.scalar.activation(out=result[:], in_=positive[:], func=ACT.Ln, bias=1.0)
+                rows = out[2 * P * q : 2 * P * (q + 1), js]
+                nc.sync.dma_start(out=rows.rearrange("(u p) j -> p u j", u=2), in_=result[:])
+
+        deal_w3(0)
+        load_w3(1, 0, "w3_raw00")
+        load_w3(1, 1, "w3_raw01")
+        prepare_w1(0, 0)
+        load_w1(1, 0)
+        linear_part(0, 0)
+        prepare_w1(0, 1)
+        load_w1(1, 1)
+        linear_part(0, 1)
+        deal_w2()
+        deal_w3(1)
+        load_duty(0, "w3_raw00")
+        load_duty(1, "w3_raw01")
+        size_part(0, 0)
+        size_part(0, 1)
+        strain(0, 0)
+        strain(0, 1)
+        prepare_w1(1, 0)
+        linear_part(1, 0)
+        prepare_w1(1, 1)
+        linear_part(1, 1)
+        crew_words(0, 0)
+        crew_words(1, 0)
+        crew_scales(0)
+        crew_words(0, 1, "w2_raw0")
+        crew_words(1, 1, "w2_raw1")
+        crew_scales(1, "w1_raw0")
+        size_part(1, 0)
+        strain(1, 0)
+        size_part(1, 1)
+        strain(1, 1)
+        banks0 = [second_early(q, 0, "second") for q in range(4)]
+        second_late(0, banks0)
+        second_late(1, [])

@@ -23,6 +23,10 @@ PASSES = K // PASS
 QUADS = 4
 CHUNK = 128
 HALF = 256
+LINE = 16
+MOVED_ROWS = 112
+VECTOR_TILES = 41
+SCALAR_TILES = 20
 
 
 def tile_list_winter_crew_friction_kernel(
@@ -33,273 +37,332 @@ def tile_list_winter_crew_friction_kernel(
         lists = ctx.enter_context(tc.tile_pool(name="lists", bufs=1))
         keep = ctx.enter_context(tc.tile_pool(name="keep", bufs=1))
         ring = ctx.enter_context(tc.tile_pool(name="ring", bufs=3))
-        psum = ctx.enter_context(tc.psum_pool(name="psum", bufs=4))
+        psum = ctx.enter_context(tc.psum_pool(name="psum", bufs=8))
 
-        def held(shape, dtype, name, tag=""):
-            return keep.tile(shape, dtype, name=name, tag=tag or name, align_bytes=64)
+        def held(shape, dtype, name, tag="", bufs=1):
+            return keep.tile(shape, dtype, name=name, tag=tag or name, bufs=bufs, align_bytes=64)
+
+        def vector_tile(shape, dtype, name):
+            return held(shape, dtype, name, "by_vector", VECTOR_TILES)
+
+        def scalar_tile(shape, dtype, name):
+            return held(shape, dtype, name, "by_scalar", SCALAR_TILES)
 
         cand_list = lists.tile([P, S // 16], U16, name="cand_list")
         crew_list = lists.tile([P, S2 // 16], U16, name="crew_list")
         tab_w = [held([P, T], I32, f"tab_w{a}") for a in range(PASSES)]
         tab_s = held([P, T], U8, "tab_s")
-        ws_raw = held([P, K], U8, "ws_raw")
+        w3s_raw = held([P, K], U8, "w3s_raw", "staged", 2)
+        w2s_raw = held([P, K], U8, "w2s_raw", "staged", 2)
         cand_s1 = held([P, S], U8, "cand_s1")
-        w2_s = [held([P, K], U8, f"w2_s{a}") for a in range(PASSES)]
+        w2_s1 = held([P, K], U8, "w2_s1")
         warm = held([P, 2], F32, "warm")
-        w1_raw = {}
-        w3_raw = {}
-        w2_raw = {}
-        duty = {}
 
-        nc.vector.memset(tab_s[:].bitcast(I32), 0)
-        nc.vector.memset(ws_raw[:].bitcast(I32), 0)
-        nc.vector.memset(cand_s1[:].bitcast(I32), 0)
-        for a in range(PASSES):
-            nc.vector.memset(w2_s[a][:].bitcast(I32), 0)
+        for zeroed in (tab_s, w3s_raw, w2s_raw, cand_s1, w2_s1):
+            nc.vector.memset(zeroed[:].bitcast(I32), 0)
         nc.vector.memset(warm[:, 0:1], 1.0)
         nc.scalar.activation(out=warm[:, 1:2], in_=warm[:, 0:1], func=ACT.Ln, bias=1.0)
+
+        w1_raw, w2_raw, w3_raw, duty = {}, {}, {}, {}
+        cand_w, crew_w, crew_s, planes = {}, {}, {}, {}
+        w1_grouped, w1_q, w2_w, w3_w = {}, {}, {}, {}
+        rounded, sizes, excess, h3_q, f_q, banks = {}, {}, {}, {}, {}, {}
 
         def load_words(tile, words):
             nc.sync.dma_start(out=tile, in_=words.rearrange("p n i -> p (n i)").bitcast(I32))
 
-        def load_scales(tile, row, scales):
+        def load_scales(tile, scales):
             for quad in range(QUADS):
                 nc.sync.dma_start(
-                    out=tile[32 * quad + row : 32 * quad + row + 8, :].bitcast(I32),
+                    out=tile[32 * quad : 32 * quad + 8, :].bitcast(I32),
                     in_=scales[:, 4 * quad : 4 * quad + 4, :].bitcast(I32),
                 )
 
-        def load_w3(b, a, tag=""):
-            w3_raw[b, a] = held([P, PASS], I32, f"w3_raw{b}{a}", tag)
-            load_words(w3_raw[b, a][:], w3_words[a][:, PASS * b : PASS * (b + 1), :])
+        def load_w3(b):
+            for a in range(PASSES):
+                w3_raw[b, a] = held([P, PASS], I32, f"w3_raw{b}{a}")
+                load_words(w3_raw[b, a][:], w3_words[a][:, PASS * b : PASS * (b + 1), :])
 
-        def load_w2(a):
-            w2_raw[a] = held([P, K // 2], I32, f"w2_raw{a}")
-            nc.sync.dma_start(out=w2_raw[a][:], in_=w2_words[a].bitcast(I32))
+        def load_w2():
+            for a in range(PASSES):
+                w2_raw[a] = held([P, K // 2], I32, f"w2_raw{a}")
+                nc.sync.dma_start(out=w2_raw[a][:], in_=w2_words[a].bitcast(I32))
 
-        def load_w1(b, a):
-            w1_raw[b, a] = held([P, PACK, PASS], F32, f"w1_raw{b}{a}", f"w1_raw{a}")
+        def load_w1(b, a, tag="", bufs=1):
+            w1_raw[b, a] = held([P, PACK, PASS], F32, f"w1_raw{b}{a}", tag, bufs)
             rows = w1[PASS * a : PASS * (a + 1), PASS * b : PASS * (b + 1)]
             nc.sync.dma_start(out=w1_raw[b, a][:], in_=rows.rearrange("(p i) c -> p i c", i=PACK))
 
-        def load_duty(g, tag):
-            duty[g] = held([P, 4, S], F32, f"duty{g}", tag)
+        def load_duty(g):
+            duty[g] = held([P, 4, S], F32, f"duty{g}", f"w2_raw{g}")
             rows = duties[4 * P * g : 4 * P * (g + 1), :]
             nc.sync.dma_start(out=duty[g][:], in_=rows.rearrange("(u p) j -> p u j", u=4))
 
-        def lower_rows(tile, source, row):
-            nc.sync.dma_start(out=tile[0 : P - row, :].bitcast(I32), in_=source[row:P, :].bitcast(I32))
+        def lower_rows(tile, source):
+            nc.sync.dma_start(
+                out=tile[0:MOVED_ROWS, :].bitcast(I32), in_=source[4 : 4 + MOVED_ROWS, :].bitcast(I32)
+            )
+
+        def gather(name, dtype, window, offsets):
+            tile = vector_tile([P, PASS], dtype, name)
+            nc.vector.tensor_copy(tile[:], window.indirect(offsets))
+            return tile
+
+        def deal(name, dtype, source, run):
+            tile = vector_tile(list(source.shape), dtype, name)
+            nc.vector.tensor_copy(
+                out=tile[:].rearrange("p (b t o i) -> p b o t i", t=PACK, i=run, o=P // run),
+                in_=source.rearrange("p (b o i t) -> p b o t i", t=PACK, i=run, o=P // run),
+            )
+            return tile
+
+        def cand_words(a):
+            cand_w[a] = gather(f"cand_w{a}", U32, tab_w[a][:].bitcast(U32), cand_list[:])
+
+        def cand_scales():
+            planes["cand"] = gather("cand_s", U8, tab_s[:], cand_list[:])
+            lower_rows(cand_s1, planes["cand"])
+
+        def crew_words(g, a):
+            offsets = crew_list[:, 32 * g : 32 * (g + 1)]
+            crew_w[g, a] = gather(f"crew_w{g}{a}", U32, tab_w[a][:].bitcast(U32), offsets)
+
+        def crew_scales(g):
+            crew_s[g] = gather(f"crew_s{g}", U8, tab_s[:], crew_list[:, 32 * g : 32 * (g + 1)])
+
+        def deal_w3(b):
+            for a in range(PASSES):
+                w3_w[b, a] = deal(f"w3_w{b}{a}", I32, w3_raw[b, a][:], LINE // 4)
+
+        def deal_w3_scales():
+            planes["w3"] = deal("w3_s", U8, w3s_raw[:], LINE)
+
+        def deal_w2_scales():
+            planes["w2"] = deal("w2_s0", U8, w2s_raw[:], LINE)
+            lower_rows(w2_s1, planes["w2"])
+
+        def deal_w2():
+            for a in range(PASSES):
+                w2_w[a] = deal(f"w2_w{a}", U16, w2_raw[a][:].bitcast(U16), LINE // 2)
+                load_duty(a)
+
+        def columns(b, t):
+            return slice(PASS * b + P * t, PASS * b + P * (t + 1))
+
+        def quantise(name, source, width):
+            codes = vector_tile([P, width], U32, name + "_w")
+            scales = held([P, width], U8, name + "_s")
+            nc.vector.quantize_mx(out=codes[:].bitcast(FP8X4), scales=scales[:], in_=source)
+            return codes, scales
+
+        def round_w1(b, a, u, engine=None):
+            source = w1_raw[b, a][:].rearrange("p i (m t) -> p m i t", t=PACK)[:, :, :, 2 * u : 2 * u + 2]
+            if engine is None:
+                grouped = scalar_tile([P, 2 * PASS], BF16, f"w1_grouped{b}{a}{u}")
+                nc.scalar.copy(out=grouped[:].rearrange("p (t m i) -> p m i t", t=2, i=PACK), in_=source)
+            else:
+                grouped = vector_tile([P, 2 * PASS], BF16, f"w1_grouped{b}{a}{u}")
+                nc.vector.tensor_copy(out=grouped[:].rearrange("p (t m i) -> p m i t", t=2, i=PACK), in_=source)
+            w1_grouped[b, a, u] = grouped
+
+        def quantise_w1(b, a, u):
+            w1_q[b, a, u] = quantise(f"w1_q{b}{a}{u}", w1_grouped[b, a, u][:], HALF)
+
+        def first_stage(c, weight, moving_scale):
+            bank = psum.tile([P, PACK, CHUNK], F32, name="bank")
+            js = slice(CHUNK * c, CHUNK * (c + 1))
+            for a in range(PASSES):
+                for t in range(PACK):
+                    lhs, lhs_scale = weight(a, t)
+                    nc.tensor.matmul_mx(
+                        out=bank[:, t, :], lhsT=lhs, lhsT_scale=lhs_scale,
+                        rhs=cand_w[a][:, js].bitcast(FP8X4), rhs_scale=moving_scale(a, js),
+                        start=(a == 0 and t == 0), stop=(a == PASSES - 1 and t == PACK - 1),
+                    )
+            return bank[:].rearrange("p t j -> p j t")
+
+        def packed_cand_scale(a, js):
+            return planes["cand"][4 * a : P, js]
+
+        def lowered_cand_scale(a, js):
+            return (planes["cand"], cand_s1)[a][:, js]
+
+        def linear_part(b, c):
+            h3 = first_stage(
+                c,
+                lambda a, t: (w3_w[b, a][:, columns(0, t)].bitcast(FP8X4), planes["w3"][4 * a : P, columns(b, t)]),
+                packed_cand_scale,
+            )
+            if c % 2 == 0:
+                rounded[b, c // 2] = scalar_tile([P, HALF, PACK], BF16, f"h3_rounded{b}{c // 2}")
+            nc.scalar.copy(out=rounded[b, c // 2][:, CHUNK * (c % 2) : CHUNK * (c % 2 + 1), :], in_=h3)
+
+        def quantise_h3(b, h):
+            h3_q[b, h] = quantise(f"h3_q{b}{h}", rounded[b, h][:].rearrange("p j t -> p (j t)"), HALF)
+
+        def size_part(b, c):
+            h1 = first_stage(
+                c,
+                lambda a, t: (
+                    w1_q[b, a, t // 2][0][:, columns(0, t % 2)].bitcast(FP8X4),
+                    w1_q[b, a, t // 2][1][:, columns(0, t % 2)],
+                ),
+                packed_cand_scale,
+            )
+            sizes[b, c] = scalar_tile([P, CHUNK, PACK], F32, f"size{b}{c}")
+            nc.scalar.activation(out=sizes[b, c][:], in_=h1, func=ACT.Abs)
+
+        def excess_part(b, c):
+            h2 = first_stage(
+                c,
+                lambda a, t: (w2_w[a][:, columns(b, t)].bitcast(FP4X4), (planes["w2"], w2_s1)[a][:, columns(b, t)]),
+                lowered_cand_scale,
+            )
+            if c % 2 == 0:
+                excess[b, c // 2] = vector_tile([P, HALF, PACK], BF16, f"excess{b}{c // 2}")
+            nc.vector.tensor_tensor(
+                out=excess[b, c // 2][:, CHUNK * (c % 2) : CHUNK * (c % 2 + 1), :],
+                in0=sizes[b, c][:], in1=h2, op=ALU.subtract,
+            )
+
+        def quantise_f(b, h):
+            clipped = vector_tile([P, HALF * PACK], BF16, f"clipped{b}{h}")
+            nc.vector.tensor_scalar(
+                out=clipped[:], in0=excess[b, h][:].rearrange("p j t -> p (j t)"),
+                scalar1=0.0, scalar2=None, op0=ALU.max,
+            )
+            f_q[b, h] = quantise(f"f_q{b}{h}", clipped[:], HALF)
+
+        def second_pass(q, h, operand, b, start=False, stop=False):
+            if start:
+                banks[q, h] = psum.tile([P, 2, HALF], F32, name="bank")
+            codes, scales = operand[b, h]
+            for u in range(2):
+                g, place = divmod(2 * q + u, 4)
+                ms = slice(P * place, P * (place + 1))
+                nc.tensor.matmul_mx(
+                    out=banks[q, h][:, u, :],
+                    lhsT=crew_w[g, b][:, ms].bitcast(FP8X4), lhsT_scale=crew_s[g][4 * b : P, ms],
+                    rhs=codes[:].bitcast(FP8X4), rhs_scale=scales[:],
+                    start=(start and u == 0), stop=(stop and u == 1),
+                )
+
+        def second_early(q, h):
+            second_pass(q, h, h3_q, 0, start=True)
+            second_pass(q, h, h3_q, 1)
+            second_pass(q, h, f_q, 0)
+
+        def second_late(q, h):
+            js = slice(HALF * h, HALF * (h + 1))
+            second_pass(q, h, f_q, 1, stop=True)
+            weighted = ring.tile([P, 2, HALF], F32, name="weighted")
+            nc.vector.tensor_tensor(
+                out=weighted[:], in0=duty[q // 2][:, 2 * (q % 2) : 2 * (q % 2) + 2, js], in1=banks[q, h][:], op=ALU.mult
+            )
+            positive = ring.tile([P, 2, HALF], F32, name="positive")
+            if q % 2 == 1:
+                nc.vector.scalar_tensor_tensor(
+                    out=positive[:], in0=weighted[:], scalar=-1.0, in1=weighted[:], op0=ALU.mult, op1=ALU.max
+                )
+            else:
+                nc.scalar.activation(out=positive[:], in_=weighted[:], func=ACT.Abs)
+            result = ring.tile([P, 2, HALF], F32, name="result", bufs=8)
+            nc.scalar.activation(out=result[:], in_=positive[:], func=ACT.Ln, bias=1.0)
+            rows = out[2 * P * q : 2 * P * (q + 1), js]
+            nc.sync.dma_start(out=rows.rearrange("(u p) j -> p u j", u=2), in_=result[:])
 
         nc.sync.dma_start(cand_list[:], offs)
         for part in range(4):
             ts = slice(PASS * part, PASS * (part + 1))
             load_words(tab_w[0][:, ts], tab_words[0][:, ts, :])
         nc.sync.dma_start(crew_list[:], offs2)
+        load_w3(0)
+        load_scales(tab_s, tab_scales)
         load_w1(0, 0)
-        load_w3(0, 0)
-        load_scales(tab_s[:], 0, tab_scales)
+        load_scales(w3s_raw, w3_scales)
         load_words(tab_w[1][:], tab_words[1])
-        load_scales(ws_raw[:], 0, w3_scales)
-        load_w3(0, 1)
-        load_scales(ws_raw[:], 8, w2_scales)
         load_w1(0, 1)
-        load_w2(0)
-        load_w2(1)
+        load_scales(w2s_raw, w2_scales)
+        load_w2()
+        load_w3(1)
 
-
-        def gather(name, width, dtype, window, offsets, tag=""):
-            tile = held([P, width], dtype, name, tag)
-            nc.vector.tensor_copy(tile[:], window.indirect(offsets))
-            return tile
-
-        def deal(name, dtype, source):
-            tile = held(list(source.shape), dtype, name)
-            nc.vector.tensor_copy(
-                out=tile[:].rearrange("p (b t m) -> p b m t", m=P, t=PACK),
-                in_=source.rearrange("p (b m t) -> p b m t", m=P, t=PACK),
-            )
-            return tile
-
-        cand_w = [None] * PASSES
-        w3_w = {}
-        cand_w[0] = gather("cand_w0", S, U32, tab_w[0][:].bitcast(U32), cand_list[:])
-        cand_s = gather("cand_s", S, U8, tab_s[:], cand_list[:])
-        lower_rows(cand_s1, cand_s, 4)
-        cand_w[1] = gather("cand_w1", S, U32, tab_w[1][:].bitcast(U32), cand_list[:])
-        ws = deal("ws", U8, ws_raw[:])
-        for a in range(PASSES):
-            lower_rows(w2_s[a], ws, 8 + 4 * a)
-
-        def deal_w3(b):
-            for a in range(PASSES):
-                w3_w[b, a] = deal(f"w3_w{b}{a}", I32, w3_raw[b, a][:])
-
-        def deal_w2():
-            for a in range(PASSES):
-                w2_w[a] = deal(f"w2_w{a}", U16, w2_raw[a][:].bitcast(U16))
-
-        def first_stage(c, weight, moving_scale):
-            bank = psum.tile([P, PACK, CHUNK], F32, name="bank", tag="first")
-            js = slice(CHUNK * c, CHUNK * (c + 1))
-            for t in range(PACK):
-                for a in range(PASSES):
-                    lhs, lhs_scale = weight(a, t)
-                    nc.tensor.matmul_mx(
-                        out=bank[:, t, :], lhsT=lhs, lhsT_scale=lhs_scale,
-                        rhs=cand_w[a][:, js].bitcast(FP8X4), rhs_scale=moving_scale(a, js),
-                        start=(a == 0), stop=(a == PASSES - 1),
-                    )
-            return bank[:].rearrange("p t j -> p j t")
-
-        def packed_cand_scale(a, js):
-            return cand_s[4 * a : P, js]
-
-        def lowered_cand_scale(a, js):
-            return (cand_s, cand_s1)[a][:, js]
-
-        def columns(b, t):
-            return slice(PASS * b + P * t, PASS * b + P * (t + 1))
-
-        def quantise(name, source, width):
-            codes = held([P, width], U32, name + "_w")
-            scales = held([P, width], U8, name + "_s")
-            nc.vector.quantize_mx(out=codes[:].bitcast(FP8X4), scales=scales[:], in_=source)
-            return codes, scales
-
-        h3_q = {}
-        f_q = {}
-        w1_q = {}
-        w2_w = [None] * PASSES
-
-        def linear_part(b, h):
-            rounded = ring.tile([P, HALF, PACK], BF16, name="h3_rounded", align_bytes=64)
-            for cc in range(2):
-                h3 = first_stage(
-                    2 * h + cc,
-                    lambda a, t: (w3_w[b, a][:, columns(0, t)].bitcast(FP8X4), ws[4 * a : P, columns(b, t)]),
-                    packed_cand_scale,
-                )
-                nc.scalar.copy(out=rounded[:, CHUNK * cc : CHUNK * (cc + 1), :], in_=h3)
-            h3_q[b, h] = quantise(f"h3_q{b}{h}", rounded[:].rearrange("p j t -> p (j t)"), HALF)
-
-        def prepare_w1(b, a):
-            grouped = ring.tile([P, PASS * PACK], BF16, name="w1_grouped", align_bytes=64)
-            nc.scalar.copy(
-                out=grouped[:].rearrange("p (t m i) -> p m i t", t=PACK, i=PACK),
-                in_=w1_raw[b, a][:].rearrange("p i (m t) -> p m i t", t=PACK),
-            )
-            w1_q[b, a] = quantise(f"w1_q{b}{a}", grouped[:], PASS)
-
-        sizes = {}
-
-        def size_part(b, h):
-            sizes[b, h] = held([P, HALF, PACK], F32, f"size{b}{h}")
-            for cc in range(2):
-                h1 = first_stage(
-                    2 * h + cc,
-                    lambda a, t: (
-                        w1_q[b, a][0][:, columns(0, t)].bitcast(FP8X4),
-                        w1_q[b, a][1][:, columns(0, t)],
-                    ),
-                    packed_cand_scale,
-                )
-                nc.scalar.activation(out=sizes[b, h][:, CHUNK * cc : CHUNK * (cc + 1), :], in_=h1, func=ACT.Abs)
-
-        def strain(b, h):
-            excess = ring.tile([P, HALF, PACK], BF16, name="excess", align_bytes=64)
-            for cc in range(2):
-                h2 = first_stage(
-                    2 * h + cc,
-                    lambda a, t: (w2_w[a][:, columns(b, t)].bitcast(FP4X4), w2_s[a][:, columns(b, t)]),
-                    lowered_cand_scale,
-                )
-                js = slice(CHUNK * cc, CHUNK * (cc + 1))
-                nc.vector.tensor_tensor(out=excess[:, js, :], in0=sizes[b, h][:, js, :], in1=h2, op=ALU.subtract)
-            clipped = ring.tile([P, HALF * PACK], BF16, name="clipped", align_bytes=64)
-            nc.vector.tensor_scalar(
-                out=clipped[:], in0=excess[:].rearrange("p j t -> p (j t)"), scalar1=0.0, scalar2=None, op0=ALU.max
-            )
-            f_q[b, h] = quantise(f"f_q{b}{h}", clipped[:], HALF)
-
-        crew_w = {}
-        crew_s = {}
-
-        def crew_words(g, a, tag=""):
-            offsets = crew_list[:, 32 * g : 32 * (g + 1)]
-            crew_w[g, a] = gather(f"crew_w{g}{a}", PASS, U32, tab_w[a][:].bitcast(U32), offsets, tag)
-
-        def crew_scales(g, tag=""):
-            crew_s[g] = gather(f"crew_s{g}", PASS, U8, tab_s[:], crew_list[:, 32 * g : 32 * (g + 1)], tag)
-
-        def second_pass(bank, q, operand, b, start, stop):
-            codes, scales = operand
-            for u in range(2):
-                g, place = divmod(2 * q + u, 4)
-                ms = slice(P * place, P * (place + 1))
-                nc.tensor.matmul_mx(
-                    out=bank[:, u, :], lhsT=crew_w[g, b][:, ms].bitcast(FP8X4), lhsT_scale=crew_s[g][4 * b : P, ms],
-                    rhs=codes[:].bitcast(FP8X4), rhs_scale=scales[:],
-                    start=(start and u == 0), stop=(stop and u == 1),
-                )
-
-        def second_early(q, h, tag):
-            bank = psum.tile([P, 2, HALF], F32, name="bank", tag=tag)
-            second_pass(bank, q, f_q[0, h], 0, True, False)
-            second_pass(bank, q, h3_q[0, h], 0, False, False)
-            second_pass(bank, q, h3_q[1, h], 1, False, False)
-            return bank
-
-        def second_late(h, banks):
-            js = slice(HALF * h, HALF * (h + 1))
-            for q in range(4):
-                if h == 1:
-                    banks.append(second_early(q, h, "first"))
-                second_pass(banks[q], q, f_q[1, h], 1, False, True)
-                weighted = ring.tile([P, 2, HALF], F32, name="weighted")
-                nc.vector.tensor_tensor(out=weighted[:], in0=duty[q // 2][:, 2 * (q % 2) : 2 * (q % 2) + 2, js], in1=banks[q][:], op=ALU.mult)
-                positive = ring.tile([P, 2, HALF], F32, name="positive")
-                if q % 2 == 1:
-                    nc.vector.scalar_tensor_tensor(
-                        out=positive[:], in0=weighted[:], scalar=-1.0, in1=weighted[:], op0=ALU.mult, op1=ALU.max
-                    )
-                else:
-                    nc.scalar.activation(out=positive[:], in_=weighted[:], func=ACT.Abs)
-                result = ring.tile([P, 2, HALF], F32, name="result", bufs=8)
-                nc.scalar.activation(out=result[:], in_=positive[:], func=ACT.Ln, bias=1.0)
-                rows = out[2 * P * q : 2 * P * (q + 1), js]
-                nc.sync.dma_start(out=rows.rearrange("(u p) j -> p u j", u=2), in_=result[:])
-
+        cand_words(0)
         deal_w3(0)
-        load_w3(1, 0, "w3_raw00")
-        load_w3(1, 1, "w3_raw01")
-        prepare_w1(0, 0)
-        load_w1(1, 0)
+        crew_words(0, 0)
+        cand_scales()
+        crew_words(1, 0)
+        round_w1(0, 0, 0)
+        round_w1(0, 0, 1)
+        deal_w3_scales()
+        load_w1(1, 0, "staged", 2)
+        crew_scales(0)
+        quantise_w1(0, 0, 0)
+        quantise_w1(0, 0, 1)
+        cand_words(1)
+        round_w1(0, 1, 0)
+        round_w1(0, 1, 1)
+        crew_words(0, 1)
+        deal_w2_scales()
+        load_w1(1, 1, "staged", 2)
+        crew_words(1, 1)
         linear_part(0, 0)
-        prepare_w1(0, 1)
-        load_w1(1, 1)
         linear_part(0, 1)
+        linear_part(0, 2)
+        linear_part(0, 3)
+        quantise_w1(0, 1, 0)
+        quantise_w1(0, 1, 1)
         deal_w2()
         deal_w3(1)
-        load_duty(0, "w3_raw00")
-        load_duty(1, "w3_raw01")
         size_part(0, 0)
         size_part(0, 1)
-        strain(0, 0)
-        strain(0, 1)
-        prepare_w1(1, 0)
+        size_part(0, 2)
+        size_part(0, 3)
+        quantise_h3(0, 0)
+        quantise_h3(0, 1)
+        crew_scales(1)
+        round_w1(1, 0, 0)
+        round_w1(1, 0, 1)
         linear_part(1, 0)
-        prepare_w1(1, 1)
         linear_part(1, 1)
-        crew_words(0, 0)
-        crew_words(1, 0)
-        crew_scales(0)
-        crew_words(0, 1, "w2_raw0")
-        crew_words(1, 1, "w2_raw1")
-        crew_scales(1, "w1_raw0")
+        excess_part(0, 0)
+        excess_part(0, 1)
+        quantise_w1(1, 0, 0)
+        quantise_w1(1, 0, 1)
+        quantise_f(0, 0)
+        round_w1(1, 1, 0)
+        round_w1(1, 1, 1)
+        linear_part(1, 2)
+        linear_part(1, 3)
+        excess_part(0, 2)
+        excess_part(0, 3)
+        quantise_w1(1, 1, 0)
+        quantise_w1(1, 1, 1)
+        quantise_f(0, 1)
+        quantise_h3(1, 0)
+        quantise_h3(1, 1)
+        second_early(0, 0)
         size_part(1, 0)
-        strain(1, 0)
+        excess_part(1, 0)
         size_part(1, 1)
-        strain(1, 1)
-        banks0 = [second_early(q, 0, "second") for q in range(4)]
-        second_late(0, banks0)
-        second_late(1, [])
+        excess_part(1, 1)
+        second_early(1, 0)
+        quantise_f(1, 0)
+        size_part(1, 2)
+        size_part(1, 3)
+        excess_part(1, 2)
+        excess_part(1, 3)
+        second_late(0, 0)
+        second_late(1, 0)
+        quantise_f(1, 1)
+        second_early(2, 0)
+        second_late(2, 0)
+        second_early(3, 0)
+        second_late(3, 0)
+        second_early(0, 1)
+        second_late(0, 1)
+        second_early(1, 1)
+        second_late(1, 1)
+        second_early(2, 1)
+        second_late(2, 1)
+        second_early(3, 1)
+        second_late(3, 1)

@@ -40,7 +40,7 @@ def tile_list_winter_crew_friction_kernel(
         psum = ctx.enter_context(tc.psum_pool(name="psum", bufs=8))
 
         def held(shape, dtype, name, tag="", bufs=1):
-            return keep.tile(shape, dtype, name=name, tag=tag or name, bufs=bufs, align_bytes=64)
+            return keep.tile(shape, dtype, name=name, tag=tag or name, bufs=bufs, align_bytes=256)
 
         def vector_tile(shape, dtype, name):
             return held(shape, dtype, name, "by_vector", VECTOR_TILES)
@@ -256,20 +256,23 @@ def tile_list_winter_crew_friction_kernel(
             js = slice(HALF * h, HALF * (h + 1))
             second_pass(q, h, f_q, 1, stop=True)
             weighted = ring.tile([P, 2, HALF], F32, name="weighted")
-            nc.vector.tensor_tensor(
-                out=weighted[:], in0=duty[q // 2][:, 2 * (q % 2) : 2 * (q % 2) + 2, js], in1=banks[q, h][:], op=ALU.mult
-            )
             positive = ring.tile([P, 2, HALF], F32, name="positive")
-            if q % 2 == 1:
-                nc.vector.scalar_tensor_tensor(
-                    out=positive[:], in0=weighted[:], scalar=-1.0, in1=weighted[:], op0=ALU.mult, op1=ALU.max
-                )
-            else:
-                nc.scalar.activation(out=positive[:], in_=weighted[:], func=ACT.Abs)
             result = ring.tile([P, 2, HALF], F32, name="result", bufs=8)
-            nc.scalar.activation(out=result[:], in_=positive[:], func=ACT.Ln, bias=1.0)
-            rows = out[2 * P * q : 2 * P * (q + 1), js]
-            nc.sync.dma_start(out=rows.rearrange("(u p) j -> p u j", u=2), in_=result[:])
+            rows = out[2 * P * q : 2 * P * (q + 1), js].rearrange("(u p) j -> p u j", u=2)
+            for us in (slice(0, 1), slice(1, 2)) if (q, h) == (3, 1) else (slice(0, 2),):
+                ds = slice(2 * (q % 2) + us.start, 2 * (q % 2) + us.stop)
+                nc.vector.tensor_tensor(
+                    out=weighted[:, us, :], in0=duty[q // 2][:, ds, js], in1=banks[q, h][:, us, :], op=ALU.mult
+                )
+                if q % 2 == 1:
+                    nc.vector.scalar_tensor_tensor(
+                        out=positive[:, us, :], in0=weighted[:, us, :], scalar=-1.0, in1=weighted[:, us, :],
+                        op0=ALU.mult, op1=ALU.max,
+                    )
+                else:
+                    nc.scalar.activation(out=positive[:, us, :], in_=weighted[:, us, :], func=ACT.Abs)
+                nc.scalar.activation(out=result[:, us, :], in_=positive[:, us, :], func=ACT.Ln, bias=1.0)
+                nc.sync.dma_start(out=rows[:, us, :], in_=result[:, us, :])
 
         nc.sync.dma_start(cand_list[:], offs)
         for part in range(4):
@@ -304,15 +307,15 @@ def tile_list_winter_crew_friction_kernel(
         crew_words(0, 1)
         deal_w2_scales()
         load_w1(1, 1, "staged", 2)
-        crew_words(1, 1)
         linear_part(0, 0)
         linear_part(0, 1)
         linear_part(0, 2)
         linear_part(0, 3)
         quantise_w1(0, 1, 0)
+        crew_words(1, 1)
         quantise_w1(0, 1, 1)
-        deal_w2()
         deal_w3(1)
+        deal_w2()
         size_part(0, 0)
         size_part(0, 1)
         size_part(0, 2)

from contextlib import ExitStack

import concourse.mybir as mybir

K, T, S, S2 = 1024, 2048, 512, 1024
FLOPS = 2 * K * K * S * 3 + 2 * S2 * K * S * 2

F32 = mybir.dt.float32
BF16 = mybir.dt.bfloat16
I32 = mybir.dt.int32
U32 = mybir.dt.uint32
U16 = mybir.dt.uint16
U8 = mybir.dt.uint8
FP8X4 = mybir.dt.float8_e4m3fn_x4
FP4X4 = mybir.dt.float4_e2m1fn_x4
ACT = mybir.ActivationFunctionType
ALU = mybir.AluOpType

P = 128
PACK = 4
PASS = P * PACK
PASSES = K // PASS
QUADS = 4
CHUNK = 128
HALF = 256
LINE = 16
MOVED_ROWS = 112
VECTOR_TILES = 41
SCALAR_TILES = 20


def tile_list_winter_crew_friction_kernel(
    tc, tab_words, tab_scales, offs, offs2, w1, w2_words, w2_scales, w3_words, w3_scales, duties, out
):
    nc = tc.nc
    with ExitStack() as ctx:
        lists = ctx.enter_context(tc.tile_pool(name="lists", bufs=1))
        keep = ctx.enter_context(tc.tile_pool(name="keep", bufs=1))
        ring = ctx.enter_context(tc.tile_pool(name="ring", bufs=3))
        psum = ctx.enter_context(tc.psum_pool(name="psum", bufs=8))

        def held(shape, dtype, name, tag="", bufs=1):
            return keep.tile(shape, dtype, name=name, tag=tag or name, bufs=bufs, align_bytes=256)

        def vector_tile(shape, dtype, name):
            return held(shape, dtype, name, "by_vector", VECTOR_TILES)

        def scalar_tile(shape, dtype, name):
            return held(shape, dtype, name, "by_scalar", SCALAR_TILES)

        cand_list = lists.tile([P, S // 16], U16, name="cand_list")
        crew_list = lists.tile([P, S2 // 16], U16, name="crew_list")
        tab_w = [held([P, T], I32, f"tab_w{a}") for a in range(PASSES)]
        tab_s = held([P, T], U8, "tab_s")
        w3s_raw = held([P, K], U8, "w3s_raw", "staged", 2)
        w2s_raw = held([P, K], U8, "w2s_raw", "staged", 2)
        cand_s1 = held([P, S], U8, "cand_s1")
        w2_s1 = held([P, K], U8, "w2_s1")
        warm = held([P, 2], F32, "warm")

        for zeroed in (tab_s, w3s_raw, w2s_raw, cand_s1, w2_s1):
            nc.vector.memset(zeroed[:].bitcast(I32), 0)
        nc.vector.memset(warm[:, 0:1], 1.0)
        nc.scalar.activation(out=warm[:, 1:2], in_=warm[:, 0:1], func=ACT.Ln, bias=1.0)

        w1_raw, w2_raw, w3_raw, duty = {}, {}, {}, {}
        cand_w, crew_w, crew_s, planes = {}, {}, {}, {}
        w1_grouped, w1_q, w2_w, w3_w = {}, {}, {}, {}
        rounded, sizes, excess, h3_q, f_q, banks = {}, {}, {}, {}, {}, {}

        def load_words(tile, words):
            nc.sync.dma_start(out=tile, in_=words.rearrange("p n i -> p (n i)").bitcast(I32))

        def load_scales(tile, scales):
            for quad in range(QUADS):
                nc.sync.dma_start(
                    out=tile[32 * quad : 32 * quad + 8, :].bitcast(I32),
                    in_=scales[:, 4 * quad : 4 * quad + 4, :].bitcast(I32),
                )

        def load_w3(b):
            for a in range(PASSES):
                w3_raw[b, a] = held([P, PASS], I32, f"w3_raw{b}{a}")
                load_words(w3_raw[b, a][:], w3_words[a][:, PASS * b : PASS * (b + 1), :])

        def load_w2():
            for a in range(PASSES):
                w2_raw[a] = held([P, K // 2], I32, f"w2_raw{a}")
                nc.sync.dma_start(out=w2_raw[a][:], in_=w2_words[a].bitcast(I32))

        def load_w1(b, a, tag="", bufs=1):
            w1_raw[b, a] = held([P, PACK, PASS], F32, f"w1_raw{b}{a}", tag, bufs)
            rows = w1[PASS * a : PASS * (a + 1), PASS * b : PASS * (b + 1)]
            nc.sync.dma_start(out=w1_raw[b, a][:], in_=rows.rearrange("(p i) c -> p i c", i=PACK))

        def load_duty(g):
            duty[g] = held([P, 4, S], F32, f"duty{g}", f"w2_raw{g}")
            rows = duties[4 * P * g : 4 * P * (g + 1), :]
            nc.sync.dma_start(out=duty[g][:], in_=rows.rearrange("(u p) j -> p u j", u=4))

        def lower_rows(tile, source):
            nc.sync.dma_start(
                out=tile[0:MOVED_ROWS, :].bitcast(I32), in_=source[4 : 4 + MOVED_ROWS, :].bitcast(I32)
            )

        def gather(name, dtype, window, offsets):
            tile = vector_tile([P, PASS], dtype, name)
            nc.vector.tensor_copy(tile[:], window.indirect(offsets))
            return tile

        def deal(name, dtype, source, run):
            tile = vector_tile(list(source.shape), dtype, name)
            nc.vector.tensor_copy(
                out=tile[:].rearrange("p (b t o i) -> p b o t i", t=PACK, i=run, o=P // run),
                in_=source.rearrange("p (b o i t) -> p b o t i", t=PACK, i=run, o=P // run),
            )
            return tile

        def cand_words(a):
            cand_w[a] = gather(f"cand_w{a}", U32, tab_w[a][:].bitcast(U32), cand_list[:])

        def cand_scales():
            planes["cand"] = gather("cand_s", U8, tab_s[:], cand_list[:])
            lower_rows(cand_s1, planes["cand"])

        def crew_words(g, a):
            offsets = crew_list[:, 32 * g : 32 * (g + 1)]
            crew_w[g, a] = gather(f"crew_w{g}{a}", U32, tab_w[a][:].bitcast(U32), offsets)

        def crew_scales(g):
            crew_s[g] = gather(f"crew_s{g}", U8, tab_s[:], crew_list[:, 32 * g : 32 * (g + 1)])

        def deal_w3(b):
            for a in range(PASSES):
                w3_w[b, a] = deal(f"w3_w{b}{a}", I32, w3_raw[b, a][:], LINE // 4)

        def deal_w3_scales():
            planes["w3"] = deal("w3_s", U8, w3s_raw[:], LINE)

        def deal_w2_scales():
            planes["w2"] = deal("w2_s0", U8, w2s_raw[:], LINE)
            lower_rows(w2_s1, planes["w2"])

        def deal_w2():
            for a in range(PASSES):
                w2_w[a] = deal(f"w2_w{a}", U16, w2_raw[a][:].bitcast(U16), LINE // 2)
                load_duty(a)

        def columns(b, t):
            return slice(PASS * b + P * t, PASS * b + P * (t + 1))

        def quantise(name, source, width):
            codes = vector_tile([P, width], U32, name + "_w")
            scales = held([P, width], U8, name + "_s")
            nc.vector.quantize_mx(out=codes[:].bitcast(FP8X4), scales=scales[:], in_=source)
            return codes, scales

        def round_w1(b, a, u, engine=None):
            source = w1_raw[b, a][:].rearrange("p i (m t) -> p m i t", t=PACK)[:, :, :, 2 * u : 2 * u + 2]
            if engine is None:
                grouped = scalar_tile([P, 2 * PASS], BF16, f"w1_grouped{b}{a}{u}")
                nc.scalar.copy(out=grouped[:].rearrange("p (t m i) -> p m i t", t=2, i=PACK), in_=source)
            else:
                grouped = vector_tile([P, 2 * PASS], BF16, f"w1_grouped{b}{a}{u}")
                nc.vector.tensor_copy(out=grouped[:].rearrange("p (t m i) -> p m i t", t=2, i=PACK), in_=source)
            w1_grouped[b, a, u] = grouped

        def quantise_w1(b, a, u):
            w1_q[b, a, u] = quantise(f"w1_q{b}{a}{u}", w1_grouped[b, a, u][:], HALF)

        def first_stage(c, weight, moving_scale):
            bank = psum.tile([P, PACK, CHUNK], F32, name="bank")
            js = slice(CHUNK * c, CHUNK * (c + 1))
            for a in range(PASSES):
                for t in range(PACK):
                    lhs, lhs_scale = weight(a, t)
                    nc.tensor.matmul_mx(
                        out=bank[:, t, :], lhsT=lhs, lhsT_scale=lhs_scale,
                        rhs=cand_w[a][:, js].bitcast(FP8X4), rhs_scale=moving_scale(a, js),
                        start=(a == 0 and t == 0), stop=(a == PASSES - 1 and t == PACK - 1),
                    )
            return bank[:].rearrange("p t j -> p j t")

        def packed_cand_scale(a, js):
            return planes["cand"][4 * a : P, js]

        def lowered_cand_scale(a, js):
            return (planes["cand"], cand_s1)[a][:, js]

        def linear_part(b, c):
            h3 = first_stage(
                c,
                lambda a, t: (w3_w[b, a][:, columns(0, t)].bitcast(FP8X4), planes["w3"][4 * a : P, columns(b, t)]),
                packed_cand_scale,
            )
            if c % 2 == 0:
                rounded[b, c // 2] = scalar_tile([P, HALF, PACK], BF16, f"h3_rounded{b}{c // 2}")
            nc.scalar.copy(out=rounded[b, c // 2][:, CHUNK * (c % 2) : CHUNK * (c % 2 + 1), :], in_=h3)

        def quantise_h3(b, h):
            h3_q[b, h] = quantise(f"h3_q{b}{h}", rounded[b, h][:].rearrange("p j t -> p (j t)"), HALF)

        def size_part(b, c):
            h1 = first_stage(
                c,
                lambda a, t: (
                    w1_q[b, a, t // 2][0][:, columns(0, t % 2)].bitcast(FP8X4),
                    w1_q[b, a, t // 2][1][:, columns(0, t % 2)],
                ),
                packed_cand_scale,
            )
            sizes[b, c] = scalar_tile([P, CHUNK, PACK], F32, f"size{b}{c}")
            nc.scalar.activation(out=sizes[b, c][:], in_=h1, func=ACT.Abs)

        def excess_part(b, c):
            h2 = first_stage(
                c,
                lambda a, t: (w2_w[a][:, columns(b, t)].bitcast(FP4X4), (planes["w2"], w2_s1)[a][:, columns(b, t)]),
                lowered_cand_scale,
            )
            if c % 2 == 0:
                excess[b, c // 2] = vector_tile([P, HALF, PACK], BF16, f"excess{b}{c // 2}")
            nc.vector.tensor_tensor(
                out=excess[b, c // 2][:, CHUNK * (c % 2) : CHUNK * (c % 2 + 1), :],
                in0=sizes[b, c][:], in1=h2, op=ALU.subtract,
            )

        def quantise_f(b, h):
            clipped = vector_tile([P, HALF * PACK], BF16, f"clipped{b}{h}")
            nc.vector.tensor_scalar(
                out=clipped[:], in0=excess[b, h][:].rearrange("p j t -> p (j t)"),
                scalar1=0.0, scalar2=None, op0=ALU.max,
            )
            f_q[b, h] = quantise(f"f_q{b}{h}", clipped[:], HALF)

        def second_pass(q, h, operand, b, start=False, stop=False):
            if start:
                banks[q, h] = psum.tile([P, 2, HALF], F32, name="bank")
            codes, scales = operand[b, h]
            for u in range(2):
                g, place = divmod(2 * q + u, 4)
                ms = slice(P * place, P * (place + 1))
                nc.tensor.matmul_mx(
                    out=banks[q, h][:, u, :],
                    lhsT=crew_w[g, b][:, ms].bitcast(FP8X4), lhsT_scale=crew_s[g][4 * b : P, ms],
                    rhs=codes[:].bitcast(FP8X4), rhs_scale=scales[:],
                    start=(start and u == 0), stop=(stop and u == 1),
                )

        def second_early(q, h):
            second_pass(q, h, h3_q, 0, start=True)
            second_pass(q, h, h3_q, 1)
            second_pass(q, h, f_q, 0)

        def second_late(q, h):
            js = slice(HALF * h, HALF * (h + 1))
            second_pass(q, h, f_q, 1, stop=True)
            weighted = ring.tile([P, 2, HALF], F32, name="weighted")
            positive = ring.tile([P, 2, HALF], F32, name="positive")
            result = ring.tile([P, 2, HALF], F32, name="result", bufs=8)
            rows = out[2 * P * q : 2 * P * (q + 1), js].rearrange("(u p) j -> p u j", u=2)
            for us in (slice(0, 1), slice(1, 2)) if (q, h) == (3, 1) else (slice(0, 2),):
                ds = slice(2 * (q % 2) + us.start, 2 * (q % 2) + us.stop)
                nc.vector.tensor_tensor(
                    out=weighted[:, us, :], in0=duty[q // 2][:, ds, js], in1=banks[q, h][:, us, :], op=ALU.mult
                )
                if q % 2 == 1:
                    nc.vector.scalar_tensor_tensor(
                        out=positive[:, us, :], in0=weighted[:, us, :], scalar=-1.0, in1=weighted[:, us, :],
                        op0=ALU.mult, op1=ALU.max,
                    )
                else:
                    nc.scalar.activation(out=positive[:, us, :], in_=weighted[:, us, :], func=ACT.Abs)
                nc.scalar.activation(out=result[:, us, :], in_=positive[:, us, :], func=ACT.Ln, bias=1.0)
                nc.sync.dma_start(out=rows[:, us, :], in_=result[:, us, :])

        nc.sync.dma_start(cand_list[:], offs)
        for part in range(4):
            ts = slice(PASS * part, PASS * (part + 1))
            load_words(tab_w[0][:, ts], tab_words[0][:, ts, :])
        nc.sync.dma_start(crew_list[:], offs2)
        load_w3(0)
        load_scales(tab_s, tab_scales)
        load_w1(0, 0)
        load_scales(w3s_raw, w3_scales)
        load_words(tab_w[1][:], tab_words[1])
        load_w1(0, 1)
        load_scales(w2s_raw, w2_scales)
        load_w2()
        load_w3(1)

        cand_words(0)
        deal_w3(0)
        crew_words(0, 0)
        cand_scales()
        crew_words(1, 0)
        round_w1(0, 0, 0)
        round_w1(0, 0, 1)
        deal_w3_scales()
        load_w1(1, 0, "staged", 2)
        crew_scales(0)
        quantise_w1(0, 0, 0)
        quantise_w1(0, 0, 1)
        cand_words(1)
        round_w1(0, 1, 0)
        round_w1(0, 1, 1)
        crew_words(0, 1)
        deal_w2_scales()
        load_w1(1, 1, "staged", 2)
        linear_part(0, 0)
        linear_part(0, 1)
        linear_part(0, 2)
        linear_part(0, 3)
        quantise_w1(0, 1, 0)
        crew_words(1, 1)
        quantise_w1(0, 1, 1)
        deal_w3(1)
        deal_w2()
        size_part(0, 0)
        size_part(0, 1)
        size_part(0, 2)
        size_part(0, 3)
        quantise_h3(0, 0)
        quantise_h3(0, 1)
        crew_scales(1)
        round_w1(1, 0, 0)
        round_w1(1, 0, 1)
        linear_part(1, 0)
        linear_part(1, 1)
        excess_part(0, 0)
        excess_part(0, 1)
        quantise_w1(1, 0, 0)
        quantise_w1(1, 0, 1)
        quantise_f(0, 0)
        round_w1(1, 1, 0)
        round_w1(1, 1, 1)
        linear_part(1, 2)
        linear_part(1, 3)
        excess_part(0, 2)
        excess_part(0, 3)
        quantise_w1(1, 1, 0)
        quantise_w1(1, 1, 1)
        quantise_f(0, 1)
        quantise_h3(1, 0)
        quantise_h3(1, 1)
        second_early(0, 0)
        size_part(1, 0)
        excess_part(1, 0)
        size_part(1, 1)
        excess_part(1, 1)
        second_early(1, 0)
        quantise_f(1, 0)
        size_part(1, 2)
        size_part(1, 3)
        excess_part(1, 2)
        excess_part(1, 3)
        second_late(0, 0)
        second_late(1, 0)
        quantise_f(1, 1)
        second_early(2, 0)
        second_late(2, 0)
        second_early(3, 0)
        second_late(3, 0)
        second_early(0, 1)
        second_late(0, 1)
        second_early(1, 1)
        second_late(1, 1)
        second_early(2, 1)
        second_late(2, 1)
        second_early(3, 1)
        second_late(3, 1)
